import numpy as np
import ml_dtypes


def mxq(x, axis, fmt="e4m3"):
    dtype, down = {"e4m3": (ml_dtypes.float8_e4m3fn, 7), "e5m2": (ml_dtypes.float8_e5m2, 14)}[fmt]
    v = np.moveaxis(np.asarray(x, np.float32).astype(ml_dtypes.bfloat16).astype(np.float64), axis, -1)
    blocks = v.reshape(v.shape[:-1] + (-1, 32))
    amax = np.abs(blocks).max(-1, keepdims=True)
    byte = np.maximum(np.where(amax > 0, np.frexp(amax)[1] - 1 + 127, 0) - down, 1)
    scale = np.exp2(byte - 127.0)
    codes = (blocks / scale).astype(np.float32).astype(dtype).astype(np.float64)
    return np.moveaxis((codes * scale).reshape(v.shape), -1, axis)


WIDE = False


def mx_kscale(k):
    if not WIDE:
        return np.ones(k)
    levels = np.array([10, -10, 5, -5, 0])
    if k % 512:
        return np.exp2(np.random.permutation(np.resize(levels, k // 32))).repeat(32)
    a = np.empty((k // 512, 16))
    for p in range(k // 512):
        a[p, :8] = np.random.permutation(np.resize(levels, 8))
        for g in range(8):
            far = levels[np.abs(levels - a[p, g]) >= 10]
            a[p, g + 8] = far[np.random.randint(len(far))]
    return np.exp2(a.ravel()).repeat(32)


def f64(x):
    return np.asarray(x).astype(np.float64)


def striped(idx):
    return np.tile(idx.reshape(-1, 16).T, (8, 1)).astype(np.uint16)


def unstriped(offs):
    return offs[:16].T.reshape(-1).astype(np.int64)


def pack_weight(w):
    k, n = w.shape
    w = f64(np.asarray(w, np.float32).astype(ml_dtypes.bfloat16)).reshape(k // 32, 32, n)
    amax = np.abs(w).max(1)
    byte = np.clip(np.where(amax > 0, np.frexp(amax)[1] - 1 + 127 - 7, 1), 1, 254)
    scaled = (w * np.exp2(127.0 - byte)[:, None, :]).reshape(k, n).astype(np.float32)
    words = np.ascontiguousarray(scaled.reshape(k // 512, 128, 4, n).transpose(0, 1, 3, 2)).astype(ml_dtypes.float8_e4m3fn).view(np.uint8)
    return words, np.ascontiguousarray(byte.astype(np.uint8).reshape(k // 512, 16, n))


def unpack_weight(words, scales):
    g, p, n, _ = words.shape
    vals = np.ascontiguousarray(words).view(ml_dtypes.float8_e4m3fn).astype(np.float64) * np.repeat(np.exp2(scales.astype(np.float64) - 127.0), 8, axis=1)[..., None]
    return vals.transpose(0, 1, 3, 2).reshape(g * 512, n)


E2M1 = np.array([0.0, 0.5, 1.0, 1.5, 2.0, 3.0, 4.0, 6.0, -0.0, -0.5, -1.0, -1.5, -2.0, -3.0, -4.0, -6.0])


def pack_fp4(w):
    k, n = w.shape
    w = f64(np.asarray(w, np.float32).astype(ml_dtypes.bfloat16)).reshape(k // 32, 32, n)
    amax = np.abs(w).max(1)
    mant, ex = np.frexp(amax / 6.0)
    byte = np.clip(np.where(amax > 0, np.where(mant > 0.5, ex, ex - 1) + 127, 1), 1, 254)
    scaled = (w * np.exp2(127.0 - byte)[:, None, :]).reshape(k, n).astype(np.float32)
    c = np.ascontiguousarray(scaled.reshape(k // 512, 128, 4, n).transpose(0, 1, 3, 2)).astype(ml_dtypes.float4_e2m1fn).view(np.uint8) & 0xF
    words = (c[..., 0::2] | (c[..., 1::2] << 4)).reshape(k // 512, 128, 2 * n)
    return np.ascontiguousarray(words), np.ascontiguousarray(byte.astype(np.uint8).reshape(k // 512, 16, n))


def unpack_fp4(words, scales):
    g, _, n = scales.shape
    words = np.ascontiguousarray(words).reshape(g, 128, n, 2)
    nib = np.empty((g, 128, n, 4), np.uint8)
    nib[..., 0::2] = words & 0xF
    nib[..., 1::2] = words >> 4
    vals = E2M1[nib] * np.repeat(np.exp2(scales.astype(np.float64) - 127.0), 8, axis=1)[..., None]
    return vals.transpose(0, 1, 3, 2).reshape(g * 512, n)


K, T, S, D, N, H = 512, 4096, 1024, 4, 128, 512


def setup_inputs():
    n = np.random.standard_normal
    s = mx_kscale(K)[:, None]
    u = mx_kscale(H)
    packed_xT = pack_weight(n((K, T)) * s)
    packed_w1 = pack_fp4(n((K, H)) / np.sqrt(K) / s)
    packed_w2 = pack_fp4(n((K, H)) / np.sqrt(K) / s)
    packed_w3 = pack_fp4(n((H, N)) / np.sqrt(H) / u[:, None])
    return {
        "x_words": packed_xT[0],
        "x_scales": packed_xT[1],
        "w1_words": packed_w1[0],
        "w1_scales": packed_w1[1],
        "w2_words": packed_w2[0],
        "w2_scales": packed_w2[1],
        "meas": (n((H, S))).astype(np.float32),
        "unit": (np.random.uniform(0.6, 1.4, (H, 1)) * u[:, None]).astype(np.float32),
        "w3_words": packed_w3[0],
        "w3_scales": packed_w3[1],
        "offs": striped(np.random.permutation(T)[:S]),
    }


def reference(x_words, x_scales, w1_words, w1_scales, w2_words, w2_scales, meas, unit, w3_words, w3_scales, offs):
    xq = unpack_weight(x_words, x_scales)[:, unstriped(offs)]
    wg = unpack_fp4(w2_words, w2_scales).T @ xq
    wei = np.log(np.exp(wg) + 1.0)
    mu = unpack_fp4(w1_words, w1_scales).T @ xq
    lik = np.exp(-1.5 * ((np.tanh(f64(meas) - mu)) ** 2))
    num = wei * lik
    den = num.reshape(len(num), -1, D).sum(axis=2) + 0.3
    upd = num / np.repeat(den, D, axis=1)
    mix = 0.2 * wei + 0.8 * upd
    hid = f64(unit) * (mix - (np.log(np.repeat(den, D, axis=1))))
    return unpack_fp4(w3_words, w3_scales).T @ mxq(hid, 0, "e4m3")

@@ -1,0 +1,292 @@
+from contextlib import ExitStack
+
+import concourse.mybir as mybir
+from concourse.masks import make_identity
+
+F32 = mybir.dt.float32
+BF16 = mybir.dt.bfloat16
+I32 = mybir.dt.int32
+U32 = mybir.dt.uint32
+U16 = mybir.dt.uint16
+U8 = mybir.dt.uint8
+FP8X4 = mybir.dt.float8_e4m3fn_x4
+FP4X4 = mybir.dt.float4_e2m1fn_x4
+ALU = mybir.AluOpType
+ACT = mybir.ActivationFunctionType
+
+K, T, S, D, N, H = 512, 4096, 1024, 4, 128, 512
+FLOPS = 2 * (2 * K * H * S + H * N * S)
+
+P = 128
+HALF = 512
+EXP_CAP = 2.0 ** 60
+
+
+def tile_picked_ygmphd_log_p_kernel(
+    tc, x_words, x_scales, w1_words, w1_scales, w2_words, w2_scales, meas, unit, w3_words, w3_scales, offs, out
+):
+    nc = tc.nc
+    with ExitStack() as ctx:
+        keep = ctx.enter_context(tc.tile_pool(name="keep", bufs=1))
+        ring = ctx.enter_context(tc.tile_pool(name="ring", bufs=4))
+        psum = ctx.enter_context(tc.psum_pool(name="psum", bufs=1))
+
+        def bank(n, name):
+            return psum.tile([P, HALF], F32, name=name, tag="bank%d" % n)
+
+        def dealt_hidden(ap):
+            return ap.rearrange("v (m t) -> v t m", t=4)
+
+        def planes(ap):
+            return ap.rearrange("v (t m) -> v t m", t=4)
+
+        offsets = keep.tile([P, S // 16], U16, name="offsets")
+        x_tab = keep.tile([P, T], U32, name="x_tab", align_bytes=64)
+        xs_tab = keep.tile([P, T], U8, name="xs_tab", tag="xs_meas", align_bytes=64)
+        w1 = keep.tile([P, 2 * H], U8, name="w1", align_bytes=64)
+        w2 = keep.tile([P, 2 * H], U8, name="w2", align_bytes=64)
+        w3 = keep.tile([P, 2 * N], U8, name="w3", align_bytes=64)
+        w1s = keep.tile([P, H], U8, name="w1s", align_bytes=64)
+        w2s = keep.tile([P, H], U8, name="w2s", align_bytes=64)
+        w3s = keep.tile([P, N], U8, name="w3s", align_bytes=64)
+        unit_sb = keep.tile([P, 4], F32, name="unit_sb")
+        unit_fifth = keep.tile([P, 4], F32, name="unit_fifth")
+        ident = keep.tile([P, P], F32, name="ident")
+        meas_sb = [None, None]
+
+        def load_scales(queue, plane, scales):
+            for q in range(4):
+                queue.dma_start(plane[32 * q : 32 * q + 4, :].bitcast(I32), scales[0, 4 * q : 4 * q + 4, :].bitcast(I32))
+
+        nc.vector.memset(xs_tab[:].bitcast(I32), 0)
+        make_identity(nc, ident[:])
+        for plane in (w2s, w1s, w3s):
+            nc.gpsimd.memset(plane[:].bitcast(I32), 0)
+        meas_rows = meas.rearrange("(q p) j -> p q j", p=P)
+        meas_sb[0] = keep.tile([P, 4, HALF], F32, name="meas0")
+        nc.sync.dma_start(offsets[:], offs)
+        nc.sync.dma_start(x_tab[:].bitcast(I32), x_words[0].rearrange("p c r -> p (c r)").bitcast(I32))
+        nc.sync.dma_start(w1[:].bitcast(I32), w1_words[0].bitcast(I32))
+        nc.sync.dma_start(meas_sb[0][:], meas_rows[:, :, 0:HALF])
+        load_scales(nc.scalar, xs_tab, x_scales)
+        nc.scalar.dma_start(w2[:].bitcast(I32), w2_words[0].bitcast(I32))
+        load_scales(nc.gpsimd, w2s, w2_scales)
+        load_scales(nc.gpsimd, w1s, w1_scales)
+        nc.scalar.dma_start(unit_sb[:], unit.rearrange("(p t) o -> p (t o)", t=4))
+        nc.scalar.mul(unit_fifth[:], unit_sb[:], 0.2)
+
+        xd, xsd = [None, None], [None, None]
+
+        def gather_scales(b):
+            picks = offsets[:, b * HALF // 16 : (b + 1) * HALF // 16]
+            gs = keep.tile([P, HALF], U8, name="gs%d" % b, align_bytes=64)
+            nc.vector.tensor_copy(gs[:], xs_tab[:].indirect(picks))
+            xsd[b] = keep.tile([P, HALF], U8, name="xsd%d" % b, align_bytes=64)
+            nc.vector.tensor_copy(xsd[b][:].rearrange("p (d v) -> p d v", d=D), gs[:].rearrange("p (v d) -> p d v", d=D))
+
+        def gather_words(b):
+            picks = offsets[:, b * HALF // 16 : (b + 1) * HALF // 16]
+            gw = keep.tile([P, HALF], U32, name="gw%d" % b, align_bytes=64)
+            nc.vector.tensor_copy(gw[:], x_tab[:].indirect(picks))
+            xd[b] = keep.tile([P, HALF], U32, name="xd%d" % b, align_bytes=64)
+            nc.vector.tensor_copy(
+                xd[b][:].bitcast(I32).rearrange("p (d v) -> p d v", d=D),
+                gw[:].bitcast(I32).rearrange("p (v d) -> p d v", d=D),
+            )
+
+        wg, wei, lik = [None] * 8, [None] * 8, [None] * 8
+        diff, diff_t, th = {}, [None] * 8, [None] * 8
+        sq = keep.tile([P, 8, HALF], F32, name="sq", tag="sq_ln")
+
+        def gate_product(k):
+            b, d = divmod(k, D)
+            cols = slice(d * P, (d + 1) * P)
+            wg[k] = bank(k, "wg%d" % k)
+            nc.tensor.matmul_mx(
+                out=wg[k][:], lhsT=xd[b][:, cols].bitcast(FP8X4), lhsT_scale=xsd[b][:, cols],
+                rhs=w2[:].bitcast(FP4X4), rhs_scale=w2s[:], start=True, stop=True,
+            )
+
+        def gate_exp(k):
+            wei[k] = keep.tile([P, HALF], F32, name="wei%d" % k)
+            nc.scalar.activation(planes(wei[k][:]), dealt_hidden(wg[k][:]), ACT.Exp)
+
+        def gate_cap(k):
+            nc.vector.tensor_scalar_min(wei[k][:], wei[k][:], EXP_CAP)
+
+        def residual(j):
+            b, h = divmod(j, 2)
+            cols = slice(h * 2 * P, (h + 1) * 2 * P)
+            for g in range(2):
+                mu = bank(4 + g, "mu%d_%d" % (j, g))
+                for q in range(2):
+                    r = 2 * g + q
+                    nc.tensor.matmul_mx(
+                        out=mu[:, q * 2 * P : (q + 1) * 2 * P],
+                        lhsT=w1[:, r * 2 * P : (r + 1) * 2 * P].bitcast(FP4X4), lhsT_scale=w1s[:, r * P : (r + 1) * P],
+                        rhs=xd[b][:, cols].bitcast(FP8X4), rhs_scale=xsd[b][:, cols], start=True, stop=True,
+                    )
+                diff[j, g] = ring.tile([P, 2, 2, P], F32, name="diff")
+                picked = meas_sb[b][:, 2 * g : 2 * g + 2, :].rearrange("p q (v d) -> p q d v", d=D)[:, :, 2 * h : 2 * h + 2, :]
+                nc.vector.tensor_sub(diff[j, g][:], picked, mu[:].rearrange("p (q d v) -> p q d v", q=2, d=2))
+
+        def turn_residual(k):
+            j, e = divmod(k, 2)
+            diff_t[k] = bank(6 + e, "diff_t%d" % k)
+            for r in range(4):
+                nc.tensor.transpose(diff_t[k][:, r * P : (r + 1) * P], diff[j, r // 2][:, r % 2, e, :], ident[:])
+
+        def tanh(k):
+            th[k] = ring.tile([P, HALF], F32, name="th")
+            nc.scalar.activation(planes(th[k][:]), dealt_hidden(diff_t[k][:]), ACT.Tanh)
+
+        def square(k):
+            nc.vector.tensor_mul(sq[:, k, :], th[k][:], th[k][:])
+
+        def likelihood(k):
+            lik[k] = keep.tile([P, HALF], F32, name="lik%d" % k)
+            nc.scalar.activation(lik[k][:], sq[:, k, :], ACT.Exp, scale=-1.5)
+
+        gather_scales(0)
+        gather_words(0)
+        gather_scales(1)
+        meas_sb[1] = keep.tile([P, 4, HALF], F32, name="meas1", tag="xs_meas", align_bytes=64)
+        nc.sync.dma_start(meas_sb[1][:], meas_rows[:, :, HALF : 2 * HALF])
+        nc.gpsimd.dma_start(w3[:].bitcast(I32), w3_words[0].bitcast(I32))
+        load_scales(nc.gpsimd, w3s, w3_scales)
+        gate_product(0)
+        gate_exp(0)
+        residual(0)
+        for k in range(1, 4):
+            gate_product(k)
+            gate_exp(k)
+        turn_residual(0)
+        turn_residual(1)
+        gather_words(1)
+        residual(1)
+        for k in range(10):
+            if k < 8:
+                tanh(k)
+                square(k)
+            if k + 2 < 8:
+                turn_residual(k + 2)
+            if k % 2 == 1 and k < 4:
+                residual(k // 2 + 2)
+            if k >= 6:
+                gate_product(k - 2)
+                gate_exp(k - 2)
+            if k >= 2:
+                likelihood(k - 2)
+        for k in range(8):
+            gate_cap(k)
+
+        soft = keep.tile([P, 8, HALF], F32, name="soft", tag="sq_ln")
+        for k in range(8):
+            nc.scalar.activation(soft[:, k, :], wei[k][:], ACT.Ln, bias=1.0)
+
+        den, inv_t, log_unit = [None, None], [None, None], [None, None]
+
+        def weight(k):
+            nc.vector.tensor_max(planes(wei[k][:]), dealt_hidden(wg[k][:]), planes(soft[:, k, :]))
+
+        def numerator(k):
+            b, d = divmod(k, D)
+            nc.vector.tensor_mul(lik[k][:], wei[k][:], lik[k][:])
+            if d == 0:
+                den[b] = bank(2 * b, "den%d" % b)
+            for t in range(4):
+                nc.tensor.matmul(
+                    den[b][:, t * P : (t + 1) * P], lhsT=lik[k][:, t * P : (t + 1) * P], rhs=ident[:],
+                    is_transpose=True, start=(d == 0 and t == 0), stop=(d == D - 1 and t == 3),
+                )
+
+        def normaliser(b):
+            log_den = keep.tile([P, HALF], F32, name="log_den%d" % b)
+            nc.scalar.activation(log_den[:], den[b][:], ACT.Ln, bias=0.3)
+            inv = keep.tile([P, HALF], F32, name="inv%d" % b)
+            nc.scalar.activation(inv[:], log_den[:], ACT.Exp, scale=-1.0)
+            inv_t[b] = bank(2 * b + 1, "inv_t%d" % b)
+            for t in range(4):
+                nc.tensor.transpose(inv_t[b][:, t * P : (t + 1) * P], inv[:, t * P : (t + 1) * P], ident[:])
+            log_unit[b] = keep.tile([P, 4, P], F32, name="log_unit%d" % b)
+            for t in range(4):
+                nc.scalar.activation(log_unit[b][:, t, :], log_den[:, t * P : (t + 1) * P], ACT.Copy, scale=unit_sb[:, t : t + 1])
+
+        result = [None, None]
+
+        mix, hids = {}, {}
+
+        def mix_part(j, g, e, term, first, last):
+            k = 2 * j + e
+            for u in range(2):
+                t = 2 * g + u
+                nc.tensor.matmul(
+                    mix[j, g][:, (2 * u + e) * P : (2 * u + e + 1) * P], lhsT=term[k][:, t * P : (t + 1) * P], rhs=ident[:],
+                    is_transpose=True, start=(first and u == 0), stop=(last and u == 1),
+                )
+
+        def open_mix(j):
+            for g in range(2):
+                mix[j, g] = bank(4 + 2 * (j % 2) + g, "mix%d_%d" % (j, g))
+                for e in range(2):
+                    mix_part(j, g, e, wei, e == 0, False)
+
+        def update(k):
+            j, e = divmod(k, 2)
+            nc.vector.scalar_tensor_tensor(lik[k][:], lik[k][:], 4.0, inv_t[k // D][:], ALU.mult, ALU.mult)
+            for g in range(2):
+                mix_part(j, g, e, lik, False, e == 1)
+
+        def hidden(j):
+            b = j // 2
+            hids[j] = ring.tile([P, 4, 2, P], BF16, name="hid")
+            for t in range(4):
+                g, u = divmod(t, 2)
+                nc.vector.scalar_tensor_tensor(
+                    hids[j][:, t, :, :], mix[j, g][:, u * 2 * P : (u + 1) * 2 * P].rearrange("p (e v) -> p e v", e=2),
+                    unit_fifth[:, t : t + 1], log_unit[b][:, t : t + 1, :].to_broadcast([P, 2, P]),
+                    ALU.mult, ALU.subtract,
+                )
+
+        def finish(j):
+            b, h = divmod(j, 2)
+            hid = hids[j]
+            woven = ring.tile([P, 2 * P, 4], BF16, name="woven", align_bytes=64)
+            src = hid[:].rearrange("p t e v -> p (e v) t")
+            if j < 3:
+                nc.scalar.copy(woven[:], src)
+            else:
+                nc.vector.tensor_copy(woven[:], src)
+            codes = ring.tile([P, 2 * P], U32, name="codes", align_bytes=64)
+            scales = ring.tile([P, 2 * P], U8, name="scales", align_bytes=64)
+            nc.vector.quantize_mx(out=codes[:].bitcast(FP8X4), scales=scales[:], in_=woven[:].rearrange("p c t -> p (c t)"))
+            if h == 0:
+                result[b] = bank(2 * b, "result%d" % b)
+            nc.tensor.matmul_mx(
+                out=result[b][:, h * 2 * P : (h + 1) * 2 * P], lhsT=w3[:].bitcast(FP4X4), lhsT_scale=w3s[:],
+                rhs=codes[:].bitcast(FP8X4), rhs_scale=scales[:], start=True, stop=True,
+            )
+            if h == 1:
+                staged = keep.tile([P, P, D], F32, name="staged%d" % b)
+                nc.scalar.copy(staged[:], result[b][:].rearrange("p (d v) -> p v d", d=D))
+                nc.sync.dma_start(out[:, b * HALF : (b + 1) * HALF], staged[:].rearrange("p v d -> p (v d)"))
+
+        weight(0)
+        for k in range(8):
+            if k < 7:
+                weight(k + 1)
+            numerator(k)
+            if k % D == D - 1:
+                normaliser(k // D)
+        for b in range(2):
+            for j in (2 * b, 2 * b + 1):
+                open_mix(j)
+            for k in range(4 * b, 4 * b + 4):
+                update(k)
+            if b == 1:
+                finish(0)
+                finish(1)
+            for j in (2 * b, 2 * b + 1):
+                hidden(j)
+        finish(2)
+        finish(3)

@@ -45,11 +45,9 @@ def tile_picked_ygmphd_log_p_kernel(
         xs_tab = keep.tile([P, T], U8, name="xs_tab", tag="xs_meas", align_bytes=64)
         w1 = keep.tile([P, 2 * H], U8, name="w1", align_bytes=64)
         w2 = keep.tile([P, 2 * H], U8, name="w2", align_bytes=64)
-        w3 = keep.tile([P, 2 * N], U8, name="w3", align_bytes=64)
         w1s = keep.tile([P, H], U8, name="w1s", align_bytes=64)
         w2s = keep.tile([P, H], U8, name="w2s", align_bytes=64)
-        w3s = keep.tile([P, N], U8, name="w3s", align_bytes=64)
-        unit_sb = keep.tile([P, 4], F32, name="unit_sb")
+        unit_sb = keep.tile([P, 4], F32, name="unit_sb", tag="unit_meas")
         unit_fifth = keep.tile([P, 4], F32, name="unit_fifth")
         ident = keep.tile([P, P], F32, name="ident")
         meas_sb = [None, None]
@@ -58,40 +56,45 @@ def tile_picked_ygmphd_log_p_kernel(
             for q in range(4):
                 queue.dma_start(plane[32 * q : 32 * q + 4, :].bitcast(I32), scales[0, 4 * q : 4 * q + 4, :].bitcast(I32))
 
-        nc.vector.memset(xs_tab[:].bitcast(I32), 0)
+        for plane in (xs_tab, w2s, w1s):
+            nc.vector.memset(plane[:].bitcast(I32), 0)
+        nc.gpsimd.dma_start(unit_sb[:], unit.rearrange("(p t) o -> p (t o)", t=4))
         make_identity(nc, ident[:])
-        for plane in (w2s, w1s, w3s):
-            nc.gpsimd.memset(plane[:].bitcast(I32), 0)
-        meas_rows = meas.rearrange("(q p) j -> p q j", p=P)
-        meas_sb[0] = keep.tile([P, 4, HALF], F32, name="meas0")
         nc.sync.dma_start(offsets[:], offs)
         nc.sync.dma_start(x_tab[:].bitcast(I32), x_words[0].rearrange("p c r -> p (c r)").bitcast(I32))
+        nc.sync.dma_start(w2[:].bitcast(I32), w2_words[0].bitcast(I32))
         nc.sync.dma_start(w1[:].bitcast(I32), w1_words[0].bitcast(I32))
-        nc.sync.dma_start(meas_sb[0][:], meas_rows[:, :, 0:HALF])
         load_scales(nc.scalar, xs_tab, x_scales)
-        nc.scalar.dma_start(w2[:].bitcast(I32), w2_words[0].bitcast(I32))
-        load_scales(nc.gpsimd, w2s, w2_scales)
-        load_scales(nc.gpsimd, w1s, w1_scales)
-        nc.scalar.dma_start(unit_sb[:], unit.rearrange("(p t) o -> p (t o)", t=4))
+        load_scales(nc.sync, w2s, w2_scales)
+        load_scales(nc.sync, w1s, w1_scales)
         nc.scalar.mul(unit_fifth[:], unit_sb[:], 0.2)
+        meas_rows = meas.rearrange("(q p) j -> p q j", p=P)
+        meas_sb[0] = keep.tile([P, 4, HALF], F32, name="meas0", tag="unit_meas")
+        nc.sync.dma_start(meas_sb[0][:], meas_rows[:, :, 0:HALF])
 
         xd, xsd = [None, None], [None, None]
 
+        gs, gw = [None, None], [None, None]
+
         def gather_scales(b):
             picks = offsets[:, b * HALF // 16 : (b + 1) * HALF // 16]
-            gs = keep.tile([P, HALF], U8, name="gs%d" % b, align_bytes=64)
-            nc.vector.tensor_copy(gs[:], xs_tab[:].indirect(picks))
+            gs[b] = keep.tile([P, HALF], U8, name="gs%d" % b, tag="picked%d" % (1 - b), align_bytes=64)
+            nc.vector.tensor_copy(gs[b][:], xs_tab[:].indirect(picks))
+
+        def deal_scales(b):
             xsd[b] = keep.tile([P, HALF], U8, name="xsd%d" % b, align_bytes=64)
-            nc.vector.tensor_copy(xsd[b][:].rearrange("p (d v) -> p d v", d=D), gs[:].rearrange("p (v d) -> p d v", d=D))
+            nc.vector.tensor_copy(xsd[b][:].rearrange("p (d v) -> p d v", d=D), gs[b][:].rearrange("p (v d) -> p d v", d=D))
 
         def gather_words(b):
             picks = offsets[:, b * HALF // 16 : (b + 1) * HALF // 16]
-            gw = keep.tile([P, HALF], U32, name="gw%d" % b, align_bytes=64)
-            nc.vector.tensor_copy(gw[:], x_tab[:].indirect(picks))
+            gw[b] = keep.tile([P, HALF], U32, name="gw%d" % b, tag="picked%d" % b, align_bytes=64)
+            nc.vector.tensor_copy(gw[b][:], x_tab[:].indirect(picks))
+
+        def deal_words(b):
             xd[b] = keep.tile([P, HALF], U32, name="xd%d" % b, align_bytes=64)
             nc.vector.tensor_copy(
-                xd[b][:].bitcast(I32).rearrange("p (d v) -> p d v", d=D),
-                gw[:].bitcast(I32).rearrange("p (v d) -> p d v", d=D),
+                xd[b][:].bitcast(I32).rearrange("p (d v) -> p v d", d=D),
+                gw[b][:].bitcast(I32).rearrange("p (v d) -> p v d", d=D),
             )
 
         wg, wei, lik = [None] * 8, [None] * 8, [None] * 8
@@ -127,8 +130,10 @@ def tile_picked_ygmphd_log_p_kernel(
                         rhs=xd[b][:, cols].bitcast(FP8X4), rhs_scale=xsd[b][:, cols], start=True, stop=True,
                     )
                 diff[j, g] = ring.tile([P, 2, 2, P], F32, name="diff")
-                picked = meas_sb[b][:, 2 * g : 2 * g + 2, :].rearrange("p q (v d) -> p q d v", d=D)[:, :, 2 * h : 2 * h + 2, :]
-                nc.vector.tensor_sub(diff[j, g][:], picked, mu[:].rearrange("p (q d v) -> p q d v", q=2, d=2))
+                picked = meas_sb[b][:, 2 * g : 2 * g + 2, :].rearrange("p q (v d) -> p q v d", d=D)[:, :, :, 2 * h : 2 * h + 2]
+                nc.vector.tensor_sub(
+                    diff[j, g][:].rearrange("p q d v -> p q v d"), picked, mu[:].rearrange("p (q d v) -> p q v d", q=2, d=2)
+                )
 
         def turn_residual(k):
             j, e = divmod(k, 2)
@@ -147,13 +152,14 @@ def tile_picked_ygmphd_log_p_kernel(
             lik[k] = keep.tile([P, HALF], F32, name="lik%d" % k)
             nc.scalar.activation(lik[k][:], sq[:, k, :], ACT.Exp, scale=-1.5)
 
-        gather_scales(0)
         gather_words(0)
+        gather_scales(0)
+        deal_words(0)
+        deal_scales(0)
         gather_scales(1)
+        deal_scales(1)
         meas_sb[1] = keep.tile([P, 4, HALF], F32, name="meas1", tag="xs_meas", align_bytes=64)
         nc.sync.dma_start(meas_sb[1][:], meas_rows[:, :, HALF : 2 * HALF])
-        nc.gpsimd.dma_start(w3[:].bitcast(I32), w3_words[0].bitcast(I32))
-        load_scales(nc.gpsimd, w3s, w3_scales)
         gate_product(0)
         gate_exp(0)
         residual(0)
@@ -163,6 +169,12 @@ def tile_picked_ygmphd_log_p_kernel(
         turn_residual(0)
         turn_residual(1)
         gather_words(1)
+        deal_words(1)
+        w3 = keep.tile([P, 2 * N], U8, name="w3", tag="picked1", align_bytes=64)
+        w3s = keep.tile([P, N], U8, name="w3s", tag="picked0", align_bytes=64)
+        nc.vector.memset(w3s[:].bitcast(I32), 0)
+        nc.sync.dma_start(w3[:].bitcast(I32), w3_words[0].bitcast(I32))
+        load_scales(nc.sync, w3s, w3_scales)
         residual(1)
         for k in range(10):
             if k < 8:
@@ -184,7 +196,7 @@ def tile_picked_ygmphd_log_p_kernel(
         for k in range(8):
             nc.scalar.activation(soft[:, k, :], wei[k][:], ACT.Ln, bias=1.0)
 
-        den, inv_t, log_unit = [None, None], [None, None], [None, None]
+        den, inv_t, log_term = [None, None], [None, None], [None, None]
 
         def weight(k):
             nc.vector.tensor_max(planes(wei[k][:]), dealt_hidden(wg[k][:]), planes(soft[:, k, :]))
@@ -208,68 +220,71 @@ def tile_picked_ygmphd_log_p_kernel(
             inv_t[b] = bank(2 * b + 1, "inv_t%d" % b)
             for t in range(4):
                 nc.tensor.transpose(inv_t[b][:, t * P : (t + 1) * P], inv[:, t * P : (t + 1) * P], ident[:])
-            log_unit[b] = keep.tile([P, 4, P], F32, name="log_unit%d" % b)
+            log_t = bank(2 * b, "log_t%d" % b)
             for t in range(4):
-                nc.scalar.activation(log_unit[b][:, t, :], log_den[:, t * P : (t + 1) * P], ACT.Copy, scale=unit_sb[:, t : t + 1])
+                nc.tensor.transpose(log_t[:, t * P : (t + 1) * P], log_den[:, t * P : (t + 1) * P], ident[:])
+            log_term[b] = keep.tile([P, HALF], F32, name="log_term%d" % b)
+            nc.scalar.mul(log_term[b][:], log_t[:], -5.0)
 
         result = [None, None]
 
-        mix, hids = {}, {}
+        mix, woven = [None] * 8, [None] * 4
 
-        def mix_part(j, g, e, term, first, last):
-            k = 2 * j + e
-            for u in range(2):
-                t = 2 * g + u
+        def add_turned(k, term, first, last):
+            for t in range(4):
                 nc.tensor.matmul(
-                    mix[j, g][:, (2 * u + e) * P : (2 * u + e + 1) * P], lhsT=term[k][:, t * P : (t + 1) * P], rhs=ident[:],
-                    is_transpose=True, start=(first and u == 0), stop=(last and u == 1),
+                    mix[k][:, t * P : (t + 1) * P], lhsT=term[:, t * P : (t + 1) * P], rhs=ident[:],
+                    is_transpose=True, start=(first and t == 0), stop=(last and t == 3),
                 )
 
-        def open_mix(j):
-            for g in range(2):
-                mix[j, g] = bank(4 + 2 * (j % 2) + g, "mix%d_%d" % (j, g))
-                for e in range(2):
-                    mix_part(j, g, e, wei, e == 0, False)
+        def open_mix(k):
+            mix[k] = bank(4 + k % D, "mix%d" % k)
+            if k % D < 2:
+                add_turned(k, wei[k], True, False)
+                add_turned(k, log_term[k // D], False, False)
+            else:
+                nc.gpsimd.tensor_add(wei[k][:], wei[k][:], log_term[k // D][:])
 
         def update(k):
-            j, e = divmod(k, 2)
             nc.vector.scalar_tensor_tensor(lik[k][:], lik[k][:], 4.0, inv_t[k // D][:], ALU.mult, ALU.mult)
-            for g in range(2):
-                mix_part(j, g, e, lik, False, e == 1)
-
-        def hidden(j):
-            b = j // 2
-            hids[j] = ring.tile([P, 4, 2, P], BF16, name="hid")
-            for t in range(4):
-                g, u = divmod(t, 2)
-                nc.vector.scalar_tensor_tensor(
-                    hids[j][:, t, :, :], mix[j, g][:, u * 2 * P : (u + 1) * 2 * P].rearrange("p (e v) -> p e v", e=2),
-                    unit_fifth[:, t : t + 1], log_unit[b][:, t : t + 1, :].to_broadcast([P, 2, P]),
-                    ALU.mult, ALU.subtract,
-                )
-
-        def finish(j):
-            b, h = divmod(j, 2)
-            hid = hids[j]
-            woven = ring.tile([P, 2 * P, 4], BF16, name="woven", align_bytes=64)
-            src = hid[:].rearrange("p t e v -> p (e v) t")
-            if j < 3:
-                nc.scalar.copy(woven[:], src)
+            if k % D < 2:
+                add_turned(k, lik[k], False, True)
             else:
-                nc.vector.tensor_copy(woven[:], src)
-            codes = ring.tile([P, 2 * P], U32, name="codes", align_bytes=64)
-            scales = ring.tile([P, 2 * P], U8, name="scales", align_bytes=64)
-            nc.vector.quantize_mx(out=codes[:].bitcast(FP8X4), scales=scales[:], in_=woven[:].rearrange("p c t -> p (c t)"))
+                add_turned(k, lik[k], True, False)
+                add_turned(k, wei[k], False, True)
+
+        def hidden(k):
+            j, e = divmod(k, 2)
+            if e == 0:
+                woven[j] = ring.tile([P, 2, P, 4], BF16, name="woven", align_bytes=64)
+            nc.vector.tensor_mul(
+                woven[j][:, e, :, :], mix[k][:].rearrange("p (t v) -> p v t", t=4),
+                unit_fifth[:].unsqueeze(1).to_broadcast([P, P, 4]),
+            )
+
+        def project(j, first, count):
+            b, h = divmod(j, 2)
+            width = count * P
+            codes = ring.tile([P, width], U32, name="codes", align_bytes=64)
+            scales = ring.tile([P, width], U8, name="scales", align_bytes=64)
+            values = woven[j][:, first : first + count, :, :].rearrange("p e v t -> p (e v t)")
+            nc.vector.quantize_mx(out=codes[:].bitcast(FP8X4), scales=scales[:], in_=values)
             if h == 0:
                 result[b] = bank(2 * b, "result%d" % b)
+            col = (2 * h + first) * P
             nc.tensor.matmul_mx(
-                out=result[b][:, h * 2 * P : (h + 1) * 2 * P], lhsT=w3[:].bitcast(FP4X4), lhsT_scale=w3s[:],
+                out=result[b][:, col : col + width], lhsT=w3[:].bitcast(FP4X4), lhsT_scale=w3s[:],
                 rhs=codes[:].bitcast(FP8X4), rhs_scale=scales[:], start=True, stop=True,
             )
-            if h == 1:
-                staged = keep.tile([P, P, D], F32, name="staged%d" % b)
-                nc.scalar.copy(staged[:], result[b][:].rearrange("p (d v) -> p v d", d=D))
-                nc.sync.dma_start(out[:, b * HALF : (b + 1) * HALF], staged[:].rearrange("p v d -> p (v d)"))
+
+        def store(b, pieces):
+            staged = keep.tile([P, P, D], F32, name="staged%d" % b)
+            groups = P // pieces
+            for n in range(pieces):
+                v = slice(n * groups, (n + 1) * groups)
+                nc.scalar.copy(staged[:, v, :], result[b][:].rearrange("p (d v) -> p v d", d=D)[:, v, :])
+                col = b * HALF + n * groups * D
+                nc.sync.dma_start(out[:, col : col + groups * D], staged[:, v, :].rearrange("p v d -> p (v d)"))
 
         weight(0)
         for k in range(8):
@@ -278,15 +293,23 @@ def tile_picked_ygmphd_log_p_kernel(
             numerator(k)
             if k % D == D - 1:
                 normaliser(k // D)
-        for b in range(2):
-            for j in (2 * b, 2 * b + 1):
-                open_mix(j)
-            for k in range(4 * b, 4 * b + 4):
-                update(k)
-            if b == 1:
-                finish(0)
-                finish(1)
-            for j in (2 * b, 2 * b + 1):
-                hidden(j)
-        finish(2)
-        finish(3)
+        for k in range(D):
+            open_mix(k)
+        for k in range(D):
+            update(k)
+        for k in range(D):
+            hidden(k)
+            open_mix(k + D)
+        project(0, 0, 2)
+        for k in range(D, 2 * D):
+            update(k)
+            if k == D:
+                project(1, 0, 2)
+                store(0, 1)
+        for k in range(D, 2 * D):
+            hidden(k)
+            if k == 2 * D - 2:
+                project(2, 0, 2)
+        project(3, 0, 1)
+        project(3, 1, 1)
+        store(1, 2)

@@ -28,7 +28,7 @@ def tile_picked_ygmphd_log_p_kernel(
     nc = tc.nc
     with ExitStack() as ctx:
         keep = ctx.enter_context(tc.tile_pool(name="keep", bufs=1))
-        ring = ctx.enter_context(tc.tile_pool(name="ring", bufs=4))
+        ring = ctx.enter_context(tc.tile_pool(name="ring", bufs=6))
         psum = ctx.enter_context(tc.psum_pool(name="psum", bufs=1))
 
         def bank(n, name):
@@ -41,13 +41,13 @@ def tile_picked_ygmphd_log_p_kernel(
             return ap.rearrange("v (t m) -> v t m", t=4)
 
         offsets = keep.tile([P, S // 16], U16, name="offsets")
-        x_tab = keep.tile([P, T], U32, name="x_tab", align_bytes=64)
+        x_tab = keep.tile([P, T], U32, name="x_tab", tag="x_tab", align_bytes=64)
         xs_tab = keep.tile([P, T], U8, name="xs_tab", tag="xs_meas", align_bytes=64)
         w1 = keep.tile([P, 2 * H], U8, name="w1", align_bytes=64)
         w2 = keep.tile([P, 2 * H], U8, name="w2", align_bytes=64)
         w1s = keep.tile([P, H], U8, name="w1s", align_bytes=64)
         w2s = keep.tile([P, H], U8, name="w2s", align_bytes=64)
-        unit_sb = keep.tile([P, 4], F32, name="unit_sb", tag="unit_meas")
+        unit_sb = keep.tile([P, 4], F32, name="unit_sb", tag="unit_meas", align_bytes=64)
         unit_fifth = keep.tile([P, 4], F32, name="unit_fifth")
         ident = keep.tile([P, P], F32, name="ident")
         meas_sb = [None, None]
@@ -61,7 +61,7 @@ def tile_picked_ygmphd_log_p_kernel(
         nc.gpsimd.dma_start(unit_sb[:], unit.rearrange("(p t) o -> p (t o)", t=4))
         make_identity(nc, ident[:])
         nc.sync.dma_start(offsets[:], offs)
-        nc.sync.dma_start(x_tab[:].bitcast(I32), x_words[0].rearrange("p c r -> p (c r)").bitcast(I32))
+        nc.sync.dma_start(x_tab[:].bitcast(I32), x_words[0].rearrange("p c r -> p (c r)").bitcast(I32), max_dma_last_dim=2048)
         nc.sync.dma_start(w2[:].bitcast(I32), w2_words[0].bitcast(I32))
         nc.sync.dma_start(w1[:].bitcast(I32), w1_words[0].bitcast(I32))
         load_scales(nc.scalar, xs_tab, x_scales)
@@ -69,7 +69,7 @@ def tile_picked_ygmphd_log_p_kernel(
         load_scales(nc.sync, w1s, w1_scales)
         nc.scalar.mul(unit_fifth[:], unit_sb[:], 0.2)
         meas_rows = meas.rearrange("(q p) j -> p q j", p=P)
-        meas_sb[0] = keep.tile([P, 4, HALF], F32, name="meas0", tag="unit_meas")
+        meas_sb[0] = keep.tile([P, 4, HALF], F32, name="meas0", tag="unit_meas", align_bytes=64)
         nc.sync.dma_start(meas_sb[0][:], meas_rows[:, :, 0:HALF])
 
         xd, xsd = [None, None], [None, None]
@@ -78,7 +78,7 @@ def tile_picked_ygmphd_log_p_kernel(
 
         def gather_scales(b):
             picks = offsets[:, b * HALF // 16 : (b + 1) * HALF // 16]
-            gs[b] = keep.tile([P, HALF], U8, name="gs%d" % b, tag="picked%d" % (1 - b), align_bytes=64)
+            gs[b] = keep.tile([P, HALF], U8, name="gs%d" % b, tag="picked", align_bytes=64)
             nc.vector.tensor_copy(gs[b][:], xs_tab[:].indirect(picks))
 
         def deal_scales(b):
@@ -87,7 +87,7 @@ def tile_picked_ygmphd_log_p_kernel(
 
         def gather_words(b):
             picks = offsets[:, b * HALF // 16 : (b + 1) * HALF // 16]
-            gw[b] = keep.tile([P, HALF], U32, name="gw%d" % b, tag="picked%d" % b, align_bytes=64)
+            gw[b] = keep.tile([P, HALF], U32, name="gw%d" % b, tag=("picked", "unit_meas")[b], align_bytes=64)
             nc.vector.tensor_copy(gw[b][:], x_tab[:].indirect(picks))
 
         def deal_words(b):
@@ -101,10 +101,10 @@ def tile_picked_ygmphd_log_p_kernel(
         diff, diff_t, th = {}, [None] * 8, [None] * 8
         sq = keep.tile([P, 8, HALF], F32, name="sq", tag="sq_ln")
 
-        def gate_product(k):
+        def gate_product(k, n, name):
             b, d = divmod(k, D)
             cols = slice(d * P, (d + 1) * P)
-            wg[k] = bank(k, "wg%d" % k)
+            wg[k] = bank(n, "%s%d" % (name, k))
             nc.tensor.matmul_mx(
                 out=wg[k][:], lhsT=xd[b][:, cols].bitcast(FP8X4), lhsT_scale=xsd[b][:, cols],
                 rhs=w2[:].bitcast(FP4X4), rhs_scale=w2s[:], start=True, stop=True,
@@ -115,13 +115,13 @@ def tile_picked_ygmphd_log_p_kernel(
             nc.scalar.activation(planes(wei[k][:]), dealt_hidden(wg[k][:]), ACT.Exp)
 
         def gate_cap(k):
-            nc.vector.tensor_scalar_min(wei[k][:], wei[k][:], EXP_CAP)
+            nc.vector.tensor_scalar_min(capped[:, k, :], wei[k][:], EXP_CAP)
 
         def residual(j):
             b, h = divmod(j, 2)
             cols = slice(h * 2 * P, (h + 1) * 2 * P)
             for g in range(2):
-                mu = bank(4 + g, "mu%d_%d" % (j, g))
+                mu = bank((4, 2, 4, 4)[j] + g, "mu%d_%d" % (j, g))
                 for q in range(2):
                     r = 2 * g + q
                     nc.tensor.matmul_mx(
@@ -137,7 +137,7 @@ def tile_picked_ygmphd_log_p_kernel(
 
         def turn_residual(k):
             j, e = divmod(k, 2)
-            diff_t[k] = bank(6 + e, "diff_t%d" % k)
+            diff_t[k] = bank((6, 7, 0, 1)[k % D], "diff_t%d" % k)
             for r in range(4):
                 nc.tensor.transpose(diff_t[k][:, r * P : (r + 1) * P], diff[j, r // 2][:, r % 2, e, :], ident[:])
 
@@ -146,57 +146,69 @@ def tile_picked_ygmphd_log_p_kernel(
             nc.scalar.activation(planes(th[k][:]), dealt_hidden(diff_t[k][:]), ACT.Tanh)
 
         def square(k):
-            nc.vector.tensor_mul(sq[:, k, :], th[k][:], th[k][:])
+            engine = nc.gpsimd if k < 4 else nc.vector
+            engine.tensor_mul(sq[:, k, :], th[k][:], th[k][:])
 
         def likelihood(k):
             lik[k] = keep.tile([P, HALF], F32, name="lik%d" % k)
             nc.scalar.activation(lik[k][:], sq[:, k, :], ACT.Exp, scale=-1.5)
 
-        gather_words(0)
         gather_scales(0)
-        deal_words(0)
         deal_scales(0)
+        gather_words(0)
+        deal_words(0)
         gather_scales(1)
         deal_scales(1)
         meas_sb[1] = keep.tile([P, 4, HALF], F32, name="meas1", tag="xs_meas", align_bytes=64)
         nc.sync.dma_start(meas_sb[1][:], meas_rows[:, :, HALF : 2 * HALF])
-        gate_product(0)
+        gate_product(0, 0, "wg")
         gate_exp(0)
         residual(0)
         for k in range(1, 4):
-            gate_product(k)
+            gate_product(k, k, "wg")
             gate_exp(k)
         turn_residual(0)
         turn_residual(1)
+        residual(1)
         gather_words(1)
         deal_words(1)
-        w3 = keep.tile([P, 2 * N], U8, name="w3", tag="picked1", align_bytes=64)
-        w3s = keep.tile([P, N], U8, name="w3s", tag="picked0", align_bytes=64)
+        w3 = keep.tile([P, 2 * N], U8, name="w3", tag="unit_meas", align_bytes=64)
+        w3s = keep.tile([P, N], U8, name="w3s", tag="x_tab", align_bytes=64)
         nc.vector.memset(w3s[:].bitcast(I32), 0)
         nc.sync.dma_start(w3[:].bitcast(I32), w3_words[0].bitcast(I32))
         load_scales(nc.sync, w3s, w3_scales)
-        residual(1)
-        for k in range(10):
+        turn_residual(2)
+        turn_residual(3)
+        for k in range(11):
             if k < 8:
                 tanh(k)
                 square(k)
-            if k + 2 < 8:
-                turn_residual(k + 2)
-            if k % 2 == 1 and k < 4:
+            if k % 2 == 0 and k < 4:
                 residual(k // 2 + 2)
-            if k >= 6:
-                gate_product(k - 2)
+            if k + 4 < 8 and k > 0:
+                turn_residual(k + 3)
+            if k == 4:
+                turn_residual(7)
+            if k >= 3:
+                likelihood(k - 3)
+            if k == 3:
+                for late in (4, 5):
+                    gate_product(late, late - 2, "wg")
+                    gate_exp(late)
+            if k in (8, 9):
+                gate_product(k - 2, k - 4, "wg")
                 gate_exp(k - 2)
-            if k >= 2:
-                likelihood(k - 2)
+        for k in range(D):
+            gate_product(k, (6, 7, 0, 1)[k], "wg_again")
+        capped = keep.tile([P, 8, HALF], F32, name="capped", tag="xs_meas", align_bytes=64)
         for k in range(8):
             gate_cap(k)
 
         soft = keep.tile([P, 8, HALF], F32, name="soft", tag="sq_ln")
         for k in range(8):
-            nc.scalar.activation(soft[:, k, :], wei[k][:], ACT.Ln, bias=1.0)
+            nc.scalar.activation(soft[:, k, :], capped[:, k, :], ACT.Ln, bias=1.0)
 
-        den, inv_t, log_term = [None, None], [None, None], [None, None]
+        den, inv_t, log_term, invs = [None, None], [None, None], [None, None], [None, None]
 
         def weight(k):
             nc.vector.tensor_max(planes(wei[k][:]), dealt_hidden(wg[k][:]), planes(soft[:, k, :]))
@@ -205,7 +217,7 @@ def tile_picked_ygmphd_log_p_kernel(
             b, d = divmod(k, D)
             nc.vector.tensor_mul(lik[k][:], wei[k][:], lik[k][:])
             if d == 0:
-                den[b] = bank(2 * b, "den%d" % b)
+                den[b] = bank((6, 0)[b], "den%d" % b)
             for t in range(4):
                 nc.tensor.matmul(
                     den[b][:, t * P : (t + 1) * P], lhsT=lik[k][:, t * P : (t + 1) * P], rhs=ident[:],
@@ -217,14 +229,18 @@ def tile_picked_ygmphd_log_p_kernel(
             nc.scalar.activation(log_den[:], den[b][:], ACT.Ln, bias=0.3)
             inv = keep.tile([P, HALF], F32, name="inv%d" % b)
             nc.scalar.activation(inv[:], log_den[:], ACT.Exp, scale=-1.0)
-            inv_t[b] = bank(2 * b + 1, "inv_t%d" % b)
-            for t in range(4):
-                nc.tensor.transpose(inv_t[b][:, t * P : (t + 1) * P], inv[:, t * P : (t + 1) * P], ident[:])
-            log_t = bank(2 * b, "log_t%d" % b)
+            invs[b] = inv
+            log_t = bank((6, 0)[b], "log_t%d" % b)
             for t in range(4):
                 nc.tensor.transpose(log_t[:, t * P : (t + 1) * P], log_den[:, t * P : (t + 1) * P], ident[:])
             log_term[b] = keep.tile([P, HALF], F32, name="log_term%d" % b)
             nc.scalar.mul(log_term[b][:], log_t[:], -5.0)
+
+        def turn_inverse(b):
+            inv = invs[b]
+            inv_t[b] = bank((7, 5)[b], "inv_t%d" % b)
+            for t in range(4):
+                nc.tensor.transpose(inv_t[b][:, t * P : (t + 1) * P], inv[:, t * P : (t + 1) * P], ident[:])
 
         result = [None, None]
 
@@ -238,7 +254,7 @@ def tile_picked_ygmphd_log_p_kernel(
                 )
 
         def open_mix(k):
-            mix[k] = bank(4 + k % D, "mix%d" % k)
+            mix[k] = bank((2, 3, 4, 5, 2, 3, 4, 7)[k], "mix%d" % k)
             if k % D < 2:
                 add_turned(k, wei[k], True, False)
                 add_turned(k, log_term[k // D], False, False)
@@ -270,7 +286,7 @@ def tile_picked_ygmphd_log_p_kernel(
             values = woven[j][:, first : first + count, :, :].rearrange("p e v t -> p (e v t)")
             nc.vector.quantize_mx(out=codes[:].bitcast(FP8X4), scales=scales[:], in_=values)
             if h == 0:
-                result[b] = bank(2 * b, "result%d" % b)
+                result[b] = bank((6, 0)[b], "result%d" % b)
             col = (2 * h + first) * P
             nc.tensor.matmul_mx(
                 out=result[b][:, col : col + width], lhsT=w3[:].bitcast(FP4X4), lhsT_scale=w3s[:],
@@ -293,19 +309,21 @@ def tile_picked_ygmphd_log_p_kernel(
             numerator(k)
             if k % D == D - 1:
                 normaliser(k // D)
+        turn_inverse(0)
         for k in range(D):
             open_mix(k)
         for k in range(D):
             update(k)
         for k in range(D):
             hidden(k)
-            open_mix(k + D)
+        turn_inverse(1)
+        for k in range(D, 2 * D):
+            open_mix(k)
         project(0, 0, 2)
+        project(1, 0, 2)
+        store(0, 1)
         for k in range(D, 2 * D):
             update(k)
-            if k == D:
-                project(1, 0, 2)
-                store(0, 1)
         for k in range(D, 2 * D):
             hidden(k)
             if k == 2 * D - 2:

from contextlib import ExitStack

import concourse.mybir as mybir
from concourse.masks import make_identity

F32 = mybir.dt.float32
BF16 = mybir.dt.bfloat16
I32 = mybir.dt.int32
U32 = mybir.dt.uint32
U16 = mybir.dt.uint16
U8 = mybir.dt.uint8
FP8X4 = mybir.dt.float8_e4m3fn_x4
FP4X4 = mybir.dt.float4_e2m1fn_x4
ALU = mybir.AluOpType
ACT = mybir.ActivationFunctionType

K, T, S, D, N, H = 512, 4096, 1024, 4, 128, 512
FLOPS = 2 * (2 * K * H * S + H * N * S)

P = 128
HALF = 512
EXP_CAP = 2.0 ** 60


def tile_picked_ygmphd_log_p_kernel(
    tc, x_words, x_scales, w1_words, w1_scales, w2_words, w2_scales, meas, unit, w3_words, w3_scales, offs, out
):
    nc = tc.nc
    with ExitStack() as ctx:
        keep = ctx.enter_context(tc.tile_pool(name="keep", bufs=1))
        ring = ctx.enter_context(tc.tile_pool(name="ring", bufs=6))
        psum = ctx.enter_context(tc.psum_pool(name="psum", bufs=1))

        def bank(n, name):
            return psum.tile([P, HALF], F32, name=name, tag="bank%d" % n)

        def dealt_hidden(ap):
            return ap.rearrange("v (m t) -> v t m", t=4)

        def planes(ap):
            return ap.rearrange("v (t m) -> v t m", t=4)

        offsets = keep.tile([P, S // 16], U16, name="offsets")
        x_tab = keep.tile([P, T], U32, name="x_tab", tag="x_tab", align_bytes=64)
        xs_tab = keep.tile([P, T], U8, name="xs_tab", tag="xs_meas", align_bytes=64)
        w1 = keep.tile([P, 2 * H], U8, name="w1", align_bytes=64)
        w2 = keep.tile([P, 2 * H], U8, name="w2", align_bytes=64)
        w1s = keep.tile([P, H], U8, name="w1s", align_bytes=64)
        w2s = keep.tile([P, H], U8, name="w2s", align_bytes=64)
        unit_sb = keep.tile([P, 4], F32, name="unit_sb", tag="unit_meas", align_bytes=64)
        unit_fifth = keep.tile([P, 4], F32, name="unit_fifth")
        ident = keep.tile([P, P], F32, name="ident")
        meas_sb = [None, None]

        def load_scales(queue, plane, scales):
            for q in range(4):
                queue.dma_start(plane[32 * q : 32 * q + 4, :].bitcast(I32), scales[0, 4 * q : 4 * q + 4, :].bitcast(I32))

        for plane in (xs_tab, w2s, w1s):
            nc.vector.memset(plane[:].bitcast(I32), 0)
        nc.gpsimd.dma_start(unit_sb[:], unit.rearrange("(p t) o -> p (t o)", t=4))
        make_identity(nc, ident[:])
        nc.sync.dma_start(offsets[:], offs)
        nc.sync.dma_start(x_tab[:].bitcast(I32), x_words[0].rearrange("p c r -> p (c r)").bitcast(I32), max_dma_last_dim=2048)
        nc.sync.dma_start(w2[:].bitcast(I32), w2_words[0].bitcast(I32))
        nc.sync.dma_start(w1[:].bitcast(I32), w1_words[0].bitcast(I32))
        load_scales(nc.scalar, xs_tab, x_scales)
        load_scales(nc.sync, w2s, w2_scales)
        load_scales(nc.sync, w1s, w1_scales)
        nc.scalar.mul(unit_fifth[:], unit_sb[:], 0.2)
        meas_rows = meas.rearrange("(q p) j -> p q j", p=P)
        meas_sb[0] = keep.tile([P, 4, HALF], F32, name="meas0", tag="unit_meas", align_bytes=64)
        nc.sync.dma_start(meas_sb[0][:], meas_rows[:, :, 0:HALF])

        xd, xsd = [None, None], [None, None]

        gs, gw = [None, None], [None, None]

        def gather_scales(b):
            picks = offsets[:, b * HALF // 16 : (b + 1) * HALF // 16]
            gs[b] = keep.tile([P, HALF], U8, name="gs%d" % b, tag="picked", align_bytes=64)
            nc.vector.tensor_copy(gs[b][:], xs_tab[:].indirect(picks))

        def deal_scales(b):
            xsd[b] = keep.tile([P, HALF], U8, name="xsd%d" % b, align_bytes=64)
            nc.vector.tensor_copy(xsd[b][:].rearrange("p (d v) -> p d v", d=D), gs[b][:].rearrange("p (v d) -> p d v", d=D))

        def gather_words(b):
            picks = offsets[:, b * HALF // 16 : (b + 1) * HALF // 16]
            gw[b] = keep.tile([P, HALF], U32, name="gw%d" % b, tag=("picked", "unit_meas")[b], align_bytes=64)
            nc.vector.tensor_copy(gw[b][:], x_tab[:].indirect(picks))

        def deal_words(b):
            xd[b] = keep.tile([P, HALF], U32, name="xd%d" % b, align_bytes=64)
            nc.vector.tensor_copy(
                xd[b][:].bitcast(I32).rearrange("p (d v) -> p v d", d=D),
                gw[b][:].bitcast(I32).rearrange("p (v d) -> p v d", d=D),
            )

        wg, wei, lik = [None] * 8, [None] * 8, [None] * 8
        diff, diff_t, th = {}, [None] * 8, [None] * 8
        sq = keep.tile([P, 8, HALF], F32, name="sq", tag="sq_ln")

        def gate_product(k, n, name):
            b, d = divmod(k, D)
            cols = slice(d * P, (d + 1) * P)
            wg[k] = bank(n, "%s%d" % (name, k))
            nc.tensor.matmul_mx(
                out=wg[k][:], lhsT=xd[b][:, cols].bitcast(FP8X4), lhsT_scale=xsd[b][:, cols],
                rhs=w2[:].bitcast(FP4X4), rhs_scale=w2s[:], start=True, stop=True,
            )

        def gate_exp(k):
            wei[k] = keep.tile([P, HALF], F32, name="wei%d" % k)
            nc.scalar.activation(planes(wei[k][:]), dealt_hidden(wg[k][:]), ACT.Exp)

        def gate_cap(k):
            nc.vector.tensor_scalar_min(capped[:, k, :], wei[k][:], EXP_CAP)

        def residual(j):
            b, h = divmod(j, 2)
            cols = slice(h * 2 * P, (h + 1) * 2 * P)
            for g in range(2):
                mu = bank((4, 2, 4, 4)[j] + g, "mu%d_%d" % (j, g))
                for q in range(2):
                    r = 2 * g + q
                    nc.tensor.matmul_mx(
                        out=mu[:, q * 2 * P : (q + 1) * 2 * P],
                        lhsT=w1[:, r * 2 * P : (r + 1) * 2 * P].bitcast(FP4X4), lhsT_scale=w1s[:, r * P : (r + 1) * P],
                        rhs=xd[b][:, cols].bitcast(FP8X4), rhs_scale=xsd[b][:, cols], start=True, stop=True,
                    )
                diff[j, g] = ring.tile([P, 2, 2, P], F32, name="diff")
                picked = meas_sb[b][:, 2 * g : 2 * g + 2, :].rearrange("p q (v d) -> p q v d", d=D)[:, :, :, 2 * h : 2 * h + 2]
                nc.vector.tensor_sub(
                    diff[j, g][:].rearrange("p q d v -> p q v d"), picked, mu[:].rearrange("p (q d v) -> p q v d", q=2, d=2)
                )

        def turn_residual(k):
            j, e = divmod(k, 2)
            diff_t[k] = bank((6, 7, 0, 1)[k % D], "diff_t%d" % k)
            for r in range(4):
                nc.tensor.transpose(diff_t[k][:, r * P : (r + 1) * P], diff[j, r // 2][:, r % 2, e, :], ident[:])

        def tanh(k):
            th[k] = ring.tile([P, HALF], F32, name="th")
            nc.scalar.activation(planes(th[k][:]), dealt_hidden(diff_t[k][:]), ACT.Tanh)

        def square(k):
            engine = nc.gpsimd if k < 4 else nc.vector
            engine.tensor_mul(sq[:, k, :], th[k][:], th[k][:])

        def likelihood(k):
            lik[k] = keep.tile([P, HALF], F32, name="lik%d" % k)
            nc.scalar.activation(lik[k][:], sq[:, k, :], ACT.Exp, scale=-1.5)

        gather_scales(0)
        deal_scales(0)
        gather_words(0)
        deal_words(0)
        gather_scales(1)
        deal_scales(1)
        meas_sb[1] = keep.tile([P, 4, HALF], F32, name="meas1", tag="xs_meas", align_bytes=64)
        nc.sync.dma_start(meas_sb[1][:], meas_rows[:, :, HALF : 2 * HALF])
        gate_product(0, 0, "wg")
        gate_exp(0)
        residual(0)
        for k in range(1, 4):
            gate_product(k, k, "wg")
            gate_exp(k)
        turn_residual(0)
        turn_residual(1)
        residual(1)
        gather_words(1)
        deal_words(1)
        w3 = keep.tile([P, 2 * N], U8, name="w3", tag="unit_meas", align_bytes=64)
        w3s = keep.tile([P, N], U8, name="w3s", tag="x_tab", align_bytes=64)
        nc.vector.memset(w3s[:].bitcast(I32), 0)
        nc.sync.dma_start(w3[:].bitcast(I32), w3_words[0].bitcast(I32))
        load_scales(nc.sync, w3s, w3_scales)
        turn_residual(2)
        turn_residual(3)
        for k in range(11):
            if k < 8:
                tanh(k)
                square(k)
            if k % 2 == 0 and k < 4:
                residual(k // 2 + 2)
            if k + 4 < 8 and k > 0:
                turn_residual(k + 3)
            if k == 4:
                turn_residual(7)
            if k >= 3:
                likelihood(k - 3)
            if k == 3:
                for late in (4, 5):
                    gate_product(late, late - 2, "wg")
                    gate_exp(late)
            if k in (8, 9):
                gate_product(k - 2, k - 4, "wg")
                gate_exp(k - 2)
        for k in range(D):
            gate_product(k, (6, 7, 0, 1)[k], "wg_again")
        capped = keep.tile([P, 8, HALF], F32, name="capped", tag="xs_meas", align_bytes=64)
        for k in range(8):
            gate_cap(k)

        soft = keep.tile([P, 8, HALF], F32, name="soft", tag="sq_ln")
        for k in range(8):
            nc.scalar.activation(soft[:, k, :], capped[:, k, :], ACT.Ln, bias=1.0)

        den, inv_t, log_term, invs = [None, None], [None, None], [None, None], [None, None]

        def weight(k):
            nc.vector.tensor_max(planes(wei[k][:]), dealt_hidden(wg[k][:]), planes(soft[:, k, :]))

        def numerator(k):
            b, d = divmod(k, D)
            nc.vector.tensor_mul(lik[k][:], wei[k][:], lik[k][:])
            if d == 0:
                den[b] = bank((6, 0)[b], "den%d" % b)
            for t in range(4):
                nc.tensor.matmul(
                    den[b][:, t * P : (t + 1) * P], lhsT=lik[k][:, t * P : (t + 1) * P], rhs=ident[:],
                    is_transpose=True, start=(d == 0 and t == 0), stop=(d == D - 1 and t == 3),
                )

        def normaliser(b):
            log_den = keep.tile([P, HALF], F32, name="log_den%d" % b)
            nc.scalar.activation(log_den[:], den[b][:], ACT.Ln, bias=0.3)
            inv = keep.tile([P, HALF], F32, name="inv%d" % b)
            nc.scalar.activation(inv[:], log_den[:], ACT.Exp, scale=-1.0)
            invs[b] = inv
            log_t = bank((6, 0)[b], "log_t%d" % b)
            for t in range(4):
                nc.tensor.transpose(log_t[:, t * P : (t + 1) * P], log_den[:, t * P : (t + 1) * P], ident[:])
            log_term[b] = keep.tile([P, HALF], F32, name="log_term%d" % b)
            nc.scalar.mul(log_term[b][:], log_t[:], -5.0)

        def turn_inverse(b):
            inv = invs[b]
            inv_t[b] = bank((7, 5)[b], "inv_t%d" % b)
            for t in range(4):
                nc.tensor.transpose(inv_t[b][:, t * P : (t + 1) * P], inv[:, t * P : (t + 1) * P], ident[:])

        result = [None, None]

        mix, woven = [None] * 8, [None] * 4

        def add_turned(k, term, first, last):
            for t in range(4):
                nc.tensor.matmul(
                    mix[k][:, t * P : (t + 1) * P], lhsT=term[:, t * P : (t + 1) * P], rhs=ident[:],
                    is_transpose=True, start=(first and t == 0), stop=(last and t == 3),
                )

        def open_mix(k):
            mix[k] = bank((2, 3, 4, 5, 2, 3, 4, 7)[k], "mix%d" % k)
            if k % D < 2:
                add_turned(k, wei[k], True, False)
                add_turned(k, log_term[k // D], False, False)
            else:
                nc.gpsimd.tensor_add(wei[k][:], wei[k][:], log_term[k // D][:])

        def update(k):
            nc.vector.scalar_tensor_tensor(lik[k][:], lik[k][:], 4.0, inv_t[k // D][:], ALU.mult, ALU.mult)
            if k % D < 2:
                add_turned(k, lik[k], False, True)
            else:
                add_turned(k, lik[k], True, False)
                add_turned(k, wei[k], False, True)

        def hidden(k):
            j, e = divmod(k, 2)
            if e == 0:
                woven[j] = ring.tile([P, 2, P, 4], BF16, name="woven", align_bytes=64)
            nc.vector.tensor_mul(
                woven[j][:, e, :, :], mix[k][:].rearrange("p (t v) -> p v t", t=4),
                unit_fifth[:].unsqueeze(1).to_broadcast([P, P, 4]),
            )

        def project(j, first, count):
            b, h = divmod(j, 2)
            width = count * P
            codes = ring.tile([P, width], U32, name="codes", align_bytes=64)
            scales = ring.tile([P, width], U8, name="scales", align_bytes=64)
            values = woven[j][:, first : first + count, :, :].rearrange("p e v t -> p (e v t)")
            nc.vector.quantize_mx(out=codes[:].bitcast(FP8X4), scales=scales[:], in_=values)
            if h == 0:
                result[b] = bank((6, 0)[b], "result%d" % b)
            col = (2 * h + first) * P
            nc.tensor.matmul_mx(
                out=result[b][:, col : col + width], lhsT=w3[:].bitcast(FP4X4), lhsT_scale=w3s[:],
                rhs=codes[:].bitcast(FP8X4), rhs_scale=scales[:], start=True, stop=True,
            )

        def store(b, pieces):
            staged = keep.tile([P, P, D], F32, name="staged%d" % b)
            groups = P // pieces
            for n in range(pieces):
                v = slice(n * groups, (n + 1) * groups)
                nc.scalar.copy(staged[:, v, :], result[b][:].rearrange("p (d v) -> p v d", d=D)[:, v, :])
                col = b * HALF + n * groups * D
                nc.sync.dma_start(out[:, col : col + groups * D], staged[:, v, :].rearrange("p v d -> p (v d)"))

        weight(0)
        for k in range(8):
            if k < 7:
                weight(k + 1)
            numerator(k)
            if k % D == D - 1:
                normaliser(k // D)
        turn_inverse(0)
        for k in range(D):
            open_mix(k)
        for k in range(D):
            update(k)
        for k in range(D):
            hidden(k)
        turn_inverse(1)
        for k in range(D, 2 * D):
            open_mix(k)
        project(0, 0, 2)
        project(1, 0, 2)
        store(0, 1)
        for k in range(D, 2 * D):
            update(k)
        for k in range(D, 2 * D):
            hidden(k)
            if k == 2 * D - 2:
                project(2, 0, 2)
        project(3, 0, 1)
        project(3, 1, 1)
        store(1, 2)
